import numpy as np
import ml_dtypes


def mxq(x, axis, fmt="e4m3"):
    dtype, down = {"e4m3": (ml_dtypes.float8_e4m3fn, 7), "e5m2": (ml_dtypes.float8_e5m2, 14)}[fmt]
    v = np.moveaxis(np.asarray(x, np.float32).astype(ml_dtypes.bfloat16).astype(np.float64), axis, -1)
    blocks = v.reshape(v.shape[:-1] + (-1, 32))
    amax = np.abs(blocks).max(-1, keepdims=True)
    byte = np.maximum(np.where(amax > 0, np.frexp(amax)[1] - 1 + 127, 0) - down, 1)
    scale = np.exp2(byte - 127.0)
    codes = (blocks / scale).astype(np.float32).astype(dtype).astype(np.float64)
    return np.moveaxis((codes * scale).reshape(v.shape), -1, axis)


WIDE = False


def mx_kscale(k):
    if not WIDE:
        return np.ones(k)
    levels = np.array([10, -10, 5, -5, 0])
    if k % 512:
        return np.exp2(np.random.permutation(np.resize(levels, k // 32))).repeat(32)
    a = np.empty((k // 512, 16))
    for p in range(k // 512):
        a[p, :8] = np.random.permutation(np.resize(levels, 8))
        for g in range(8):
            far = levels[np.abs(levels - a[p, g]) >= 10]
            a[p, g + 8] = far[np.random.randint(len(far))]
    return np.exp2(a.ravel()).repeat(32)


def f64(x):
    return np.asarray(x).astype(np.float64)


def striped(idx):
    return np.tile(idx.reshape(-1, 16).T, (8, 1)).astype(np.uint16)


def unstriped(offs):
    return offs[:16].T.reshape(-1).astype(np.int64)


def pack_weight(w):
    k, n = w.shape
    w = f64(np.asarray(w, np.float32).astype(ml_dtypes.bfloat16)).reshape(k // 32, 32, n)
    amax = np.abs(w).max(1)
    byte = np.clip(np.where(amax > 0, np.frexp(amax)[1] - 1 + 127 - 7, 1), 1, 254)
    scaled = (w * np.exp2(127.0 - byte)[:, None, :]).reshape(k, n).astype(np.float32)
    words = np.ascontiguousarray(scaled.reshape(k // 512, 128, 4, n).transpose(0, 1, 3, 2)).astype(ml_dtypes.float8_e4m3fn).view(np.uint8)
    return words, np.ascontiguousarray(byte.astype(np.uint8).reshape(k // 512, 16, n))


def unpack_weight(words, scales):
    g, p, n, _ = words.shape
    vals = np.ascontiguousarray(words).view(ml_dtypes.float8_e4m3fn).astype(np.float64) * np.repeat(np.exp2(scales.astype(np.float64) - 127.0), 8, axis=1)[..., None]
    return vals.transpose(0, 1, 3, 2).reshape(g * 512, n)


def gelu(v):
    return 0.5 * v * (1.0 + np.tanh(np.sqrt(2.0 / np.pi) * (v + 0.044715 * v**3)))


K, T, E, C, N = 1024, 512, 8, 128, 256


def by_expert(wq, xq):
    return np.concatenate([wq[e].T @ xq[:, e * C:(e + 1) * C] for e in range(E)], axis=1)


def setup_inputs():
    n = np.random.standard_normal
    s = mx_kscale(K)[:, None]
    first = np.random.permutation(np.repeat(np.arange(E), T // E))
    second = (first + 1 + np.random.permutation(np.repeat(np.arange(E - 1), -(-T // (E - 1)))[:T])) % E
    while np.bincount(second, minlength=E).max() != T // E:
        load = np.bincount(second, minlength=E); hi, lo = int(load.argmax()), int(load.argmin())
        t = np.flatnonzero((second == hi) & (first != lo))[0]; second[t] = lo
    slot_token = np.empty(E * C, np.int64); pos = np.empty((2, T), np.int64); fill = np.zeros(E, np.int64)
    place = np.stack([np.random.permutation(C) for _ in range(E)])
    for r, deal in enumerate((first, second)):
        for t in np.random.permutation(T):
            e = deal[t]; j = e * C + place[e, fill[e]]; fill[e] += 1; slot_token[j] = t; pos[r, t] = j
    g = np.random.uniform(0.2, 0.8, T)
    packed = [pack_weight(m) for m in n((E, K, N)) / np.sqrt(K) / s[None]]
    return {
        "xT": (n((K, T)) * s).astype(np.float32),
        "w_words": np.stack([m[0] for m in packed]),
        "w_scales": np.stack([m[1] for m in packed]),
        "b": (0.3 * n((N, E))).astype(np.float32),
        "gate": np.stack([np.tile(g, (N, 1)), np.tile(1.0 - g, (N, 1))]).astype(np.float32),
        "offs": striped(slot_token),
        "pos1": striped(pos[0]),
        "pos2": striped(pos[1]),
    }


def reference(xT, w_words, w_scales, b, gate, offs, pos1, pos2):
    idx = unstriped(offs)
    xq = mxq(f64(xT)[:, idx], 0, "e4m3")
    w = np.stack([unpack_weight(w_words[e], w_scales[e]) for e in range(E)])
    y = by_expert(w, xq)
    y = gelu(y + np.repeat(f64(b), C, axis=1))
    return f64(gate[0]) * y[:, unstriped(pos1)] + f64(gate[1]) * y[:, unstriped(pos2)]

@@ -1,0 +1,146 @@
+from contextlib import ExitStack
+
+import concourse.mybir as mybir
+
+K, T, E, C, N = 1024, 512, 8, 128, 256
+FLOPS = 2 * K * N * E * C
+
+F32 = mybir.dt.float32
+BF16 = mybir.dt.bfloat16
+U32 = mybir.dt.uint32
+I32 = mybir.dt.int32
+U16 = mybir.dt.uint16
+U8 = mybir.dt.uint8
+FP8X4 = mybir.dt.float8_e4m3fn_x4
+ACT = mybir.ActivationFunctionType
+MULT = mybir.AluOpType.mult
+
+P = 128
+PACK = 4
+PASSES = K // (P * PACK)
+BLOCKS = N // P
+HALF = T // 2
+SLOTS = E * C
+PIECES = ((0, 3), (3, 6), (6, 8))
+
+
+def tile_routed_moe_kernel(tc, xT, w_words, w_scales, b, gate, offs, pos1, pos2, out):
+    nc = tc.nc
+    with ExitStack() as ctx:
+        keep = ctx.enter_context(tc.tile_pool(name="keep", bufs=1))
+        psum = ctx.enter_context(tc.psum_pool(name="psum", bufs=8))
+
+        offs_t = keep.tile([P, SLOTS // 16], U16, name="offs_t")
+        pos1_t = keep.tile([P, T // 16], U16, name="pos1_t")
+        pos2_t = keep.tile([P, T // 16], U16, name="pos2_t")
+        bias = keep.tile([P, BLOCKS, E], F32, name="bias")
+        w_codes = keep.tile([P, E * PASSES, N], U32, name="w_codes", align_bytes=64)
+        w_planes = keep.tile([P, E * PASSES, N], U8, name="w_planes", align_bytes=64)
+        x_planes = keep.tile([P, T], U8, name="x_planes", align_bytes=64)
+        slot_planes = keep.tile([P, SLOTS], U8, name="slot_planes", align_bytes=64)
+
+        warm = keep.tile([P, 1], F32, name="warm")
+        nc.gpsimd.memset(warm[:], 0.0)
+        warmed = keep.tile([P, 1], F32, name="warmed")
+        nc.scalar.activation(warmed[:], warm[:], ACT.Gelu_apprx_tanh)
+
+        nc.gpsimd.memset(x_planes[:], 0)
+        nc.vector.memset(w_planes[:].rearrange("p g n -> p (g n)").bitcast(I32), 0)
+
+        xv = xT.rearrange("(a p j) t -> a p j t", p=P, j=PACK)
+        raw = []
+        for a in range(PASSES):
+            halves = []
+            for h in range(2):
+                r = keep.tile([P, PACK, HALF], F32, name=f"raw{a}{h}")
+                nc.sync.dma_start(out=r[:], in_=xv[a, :, :, h * HALF : (h + 1) * HALF])
+                halves.append(r)
+            raw.append(halves)
+            if a == 0:
+                nc.sync.dma_start(offs_t[:], offs)
+
+        wsv = w_scales.rearrange("e a q n -> q (e a) n")
+        for quad in range(4):
+            nc.sync.dma_start(
+                out=w_planes[32 * quad : 32 * quad + 4, :, :].bitcast(I32),
+                in_=wsv[4 * quad : 4 * quad + 4].bitcast(I32),
+            )
+        wwv = w_words.rearrange("e a p n r -> p (e a) (n r)")
+        for e0, e1 in PIECES:
+            nc.sync.dma_start(
+                out=w_codes[:, e0 * PASSES : e1 * PASSES, :].bitcast(I32),
+                in_=wwv[:, e0 * PASSES : e1 * PASSES, :].bitcast(I32),
+            )
+            if e0 == 0:
+                nc.sync.dma_start(out=bias[:], in_=b.rearrange("(m p) e -> p m e", p=P))
+        nc.sync.dma_start(pos1_t[:], pos1)
+        nc.sync.dma_start(pos2_t[:], pos2)
+        gates = []
+        for m in range(BLOCKS):
+            g = keep.tile([P, 2, T], F32, name=f"gate{m}")
+            nc.sync.dma_start(out=g[:], in_=gate[:, m * P : (m + 1) * P, :].rearrange("r p t -> p r t"))
+            gates.append(g)
+
+        x_bf = [keep.tile([P, T, PACK], BF16, name=f"x_bf{a}", align_bytes=64) for a in range(PASSES)]
+        x_codes = [keep.tile([P, T], U32, name=f"x_codes{a}", align_bytes=64) for a in range(PASSES)]
+        slot_codes = [keep.tile([P, SLOTS], U32, name=f"slot_codes{a}", align_bytes=64) for a in range(PASSES)]
+
+        def interleave(copy, a, h, lo, hi):
+            copy(
+                out=x_bf[a][:, h * HALF + lo : h * HALF + hi, :],
+                in_=raw[a][h][:, :, lo:hi].rearrange("p j t -> p t j"),
+            )
+
+        def quantise(a, lo, hi):
+            nc.vector.quantize_mx(
+                out=x_codes[a][:, lo:hi].bitcast(FP8X4),
+                scales=x_planes[4 * a : P, lo:hi],
+                in_=x_bf[a][:, lo:hi, :].rearrange("p t j -> p (t j)"),
+            )
+
+        def gather(dst, src, e0, e1):
+            nc.vector.tensor_copy(
+                out=dst[:, e0 * C : e1 * C],
+                in_=src[:].indirect(offs_t[:, e0 * C // 16 : e1 * C // 16]),
+            )
+
+        interleave(nc.vector.tensor_copy, 0, 0, 0, HALF)
+        quantise(0, 0, HALF)
+        interleave(nc.vector.tensor_copy, 0, 1, 0, 160)
+        interleave(nc.scalar.copy, 0, 1, 160, HALF)
+        quantise(0, HALF, T)
+        interleave(nc.scalar.copy, 1, 0, 0, HALF)
+        interleave(nc.scalar.copy, 1, 1, 0, HALF)
+        for e0, e1 in PIECES:
+            gather(slot_codes[0], x_codes[0], e0, e1)
+        quantise(1, 0, T)
+
+        y = [keep.tile([P, SLOTS], F32, name=f"y{m}") for m in range(BLOCKS)]
+        for e0, e1 in PIECES:
+            gather(slot_planes, x_planes, e0, e1)
+            gather(slot_codes[1], x_codes[1], e0, e1)
+            for m in range(BLOCKS):
+                for e in range(e0, e1):
+                    slots = slice(e * C, (e + 1) * C)
+                    rows = slice(m * P, (m + 1) * P)
+                    acc = psum.tile([P, C], F32, name="acc")
+                    for a in range(PASSES):
+                        nc.tensor.matmul_mx(
+                            out=acc[:],
+                            lhsT=w_codes[:, e * PASSES + a, rows].bitcast(FP8X4),
+                            lhsT_scale=w_planes[:, e * PASSES + a, rows],
+                            rhs=slot_codes[a][:, slots].bitcast(FP8X4),
+                            rhs_scale=slot_planes[4 * a : P, slots],
+                            start=(a == 0),
+                            stop=(a == PASSES - 1),
+                        )
+                    nc.scalar.activation(y[m][:, slots], acc[:], ACT.Gelu_apprx_tanh, bias=bias[:, m, e : e + 1])
+
+        for m in range(BLOCKS):
+            first = keep.tile([P, T], F32, name=f"first{m}")
+            second = keep.tile([P, T], F32, name=f"second{m}")
+            total = keep.tile([P, T], F32, name=f"total{m}")
+            nc.vector.tensor_tensor(first[:], y[m][:].indirect(pos1_t[:]), gates[m][:, 0, :], MULT)
+            nc.vector.tensor_tensor(second[:], y[m][:].indirect(pos2_t[:]), gates[m][:, 1, :], MULT)
+            nc.vector.tensor_add(total[:], first[:], second[:])
+            nc.sync.dma_start(out=out[m * P : (m + 1) * P, :], in_=total[:])

@@ -1,6 +1,7 @@
 from contextlib import ExitStack
 
 import concourse.mybir as mybir
+from concourse.masks import make_identity
 
 K, T, E, C, N = 1024, 512, 8, 128, 256
 FLOPS = 2 * K * N * E * C
@@ -21,6 +22,7 @@ PASSES = K // (P * PACK)
 BLOCKS = N // P
 HALF = T // 2
 SLOTS = E * C
+CHUNKS = (((0, 384), (384, 512)), ((0, 256), (256, 512)))
 PIECES = ((0, 3), (3, 6), (6, 8))
 
 
@@ -28,7 +30,8 @@ def tile_routed_moe_kernel(tc, xT, w_words, w_scales, b, gate, offs, pos1, pos2,
     nc = tc.nc
     with ExitStack() as ctx:
         keep = ctx.enter_context(tc.tile_pool(name="keep", bufs=1))
-        psum = ctx.enter_context(tc.psum_pool(name="psum", bufs=8))
+        psum = ctx.enter_context(tc.psum_pool(name="psum", bufs=6))
+        sums = ctx.enter_context(tc.psum_pool(name="sums", bufs=2))
 
         offs_t = keep.tile([P, SLOTS // 16], U16, name="offs_t")
         pos1_t = keep.tile([P, T // 16], U16, name="pos1_t")
@@ -45,17 +48,19 @@ def tile_routed_moe_kernel(tc, xT, w_words, w_scales, b, gate, offs, pos1, pos2,
         nc.scalar.activation(warmed[:], warm[:], ACT.Gelu_apprx_tanh)
 
         nc.gpsimd.memset(x_planes[:], 0)
+        identity = keep.tile([P, P], F32, name="identity")
+        make_identity(nc, identity[:])
         nc.vector.memset(w_planes[:].rearrange("p g n -> p (g n)").bitcast(I32), 0)
 
         xv = xT.rearrange("(a p j) t -> a p j t", p=P, j=PACK)
         raw = []
         for a in range(PASSES):
-            halves = []
-            for h in range(2):
-                r = keep.tile([P, PACK, HALF], F32, name=f"raw{a}{h}")
-                nc.sync.dma_start(out=r[:], in_=xv[a, :, :, h * HALF : (h + 1) * HALF])
-                halves.append(r)
-            raw.append(halves)
+            chunks = []
+            for lo, hi in CHUNKS[a]:
+                r = keep.tile([P, PACK, hi - lo], F32, name=f"raw{a}_{lo}")
+                nc.sync.dma_start(out=r[:], in_=xv[a, :, :, lo:hi])
+                chunks.append(r)
+            raw.append(chunks)
             if a == 0:
                 nc.sync.dma_start(offs_t[:], offs)
 
@@ -86,9 +91,10 @@ def tile_routed_moe_kernel(tc, xT, w_words, w_scales, b, gate, offs, pos1, pos2,
         slot_codes = [keep.tile([P, SLOTS], U32, name=f"slot_codes{a}", align_bytes=64) for a in range(PASSES)]
 
         def interleave(copy, a, h, lo, hi):
+            start = CHUNKS[a][h][0]
             copy(
-                out=x_bf[a][:, h * HALF + lo : h * HALF + hi, :],
-                in_=raw[a][h][:, :, lo:hi].rearrange("p j t -> p t j"),
+                out=x_bf[a][:, lo:hi, :].rearrange("p (c i) j -> p c j i", i=4),
+                in_=raw[a][h][:, :, lo - start : hi - start].rearrange("p j (c i) -> p c j i", i=4),
             )
 
         def quantise(a, lo, hi):
@@ -104,43 +110,74 @@ def tile_routed_moe_kernel(tc, xT, w_words, w_scales, b, gate, offs, pos1, pos2,
                 in_=src[:].indirect(offs_t[:, e0 * C // 16 : e1 * C // 16]),
             )
 
-        interleave(nc.vector.tensor_copy, 0, 0, 0, HALF)
-        quantise(0, 0, HALF)
-        interleave(nc.vector.tensor_copy, 0, 1, 0, 160)
-        interleave(nc.scalar.copy, 0, 1, 160, HALF)
-        quantise(0, HALF, T)
-        interleave(nc.scalar.copy, 1, 0, 0, HALF)
-        interleave(nc.scalar.copy, 1, 1, 0, HALF)
+        interleave(nc.vector.tensor_copy, 0, 0, 0, 256)
+        interleave(nc.scalar.copy, 0, 0, 256, 384)
+        quantise(0, 0, 256)
+        quantise(0, 256, 384)
+        interleave(nc.vector.tensor_copy, 0, 1, 384, 464)
+        interleave(nc.scalar.copy, 0, 1, 464, 512)
+        quantise(0, 384, 512)
+        interleave(nc.scalar.copy, 1, 0, 0, 256)
+        interleave(nc.scalar.copy, 1, 1, 256, 512)
         for e0, e1 in PIECES:
             gather(slot_codes[0], x_codes[0], e0, e1)
-        quantise(1, 0, T)
+        quantise(1, 0, HALF)
+        quantise(1, HALF, T)
 
         y = [keep.tile([P, SLOTS], F32, name=f"y{m}") for m in range(BLOCKS)]
         for e0, e1 in PIECES:
             gather(slot_planes, x_planes, e0, e1)
             gather(slot_codes[1], x_codes[1], e0, e1)
-            for m in range(BLOCKS):
-                for e in range(e0, e1):
+            groups = [(m, e) for m in range(BLOCKS) for e in range(e0, e1)]
+            banks = {}
+            for a in range(PASSES):
+                for m, e in groups:
                     slots = slice(e * C, (e + 1) * C)
                     rows = slice(m * P, (m + 1) * P)
-                    acc = psum.tile([P, C], F32, name="acc")
-                    for a in range(PASSES):
-                        nc.tensor.matmul_mx(
-                            out=acc[:],
-                            lhsT=w_codes[:, e * PASSES + a, rows].bitcast(FP8X4),
-                            lhsT_scale=w_planes[:, e * PASSES + a, rows],
-                            rhs=slot_codes[a][:, slots].bitcast(FP8X4),
-                            rhs_scale=slot_planes[4 * a : P, slots],
-                            start=(a == 0),
-                            stop=(a == PASSES - 1),
-                        )
-                    nc.scalar.activation(y[m][:, slots], acc[:], ACT.Gelu_apprx_tanh, bias=bias[:, m, e : e + 1])
+                    if a == 0:
+                        banks[m, e] = psum.tile([P, C], F32, name="acc")
+                    nc.tensor.matmul_mx(
+                        out=banks[m, e][:],
+                        lhsT=w_codes[:, e * PASSES + a, rows].bitcast(FP8X4),
+                        lhsT_scale=w_planes[:, e * PASSES + a, rows],
+                        rhs=slot_codes[a][:, slots].bitcast(FP8X4),
+                        rhs_scale=slot_planes[4 * a : P, slots],
+                        start=(a == 0),
+                        stop=(a == PASSES - 1),
+                    )
+            for m, e in groups:
+                slots = slice(e * C, (e + 1) * C)
+                nc.scalar.activation(y[m][:, slots], banks[m, e][:], ACT.Gelu_apprx_tanh, bias=bias[:, m, e : e + 1])
 
+        halves = [slice(h * HALF, (h + 1) * HALF) for h in range(2)]
+        products = []
         for m in range(BLOCKS):
             first = keep.tile([P, T], F32, name=f"first{m}")
             second = keep.tile([P, T], F32, name=f"second{m}")
-            total = keep.tile([P, T], F32, name=f"total{m}")
             nc.vector.tensor_tensor(first[:], y[m][:].indirect(pos1_t[:]), gates[m][:, 0, :], MULT)
-            nc.vector.tensor_tensor(second[:], y[m][:].indirect(pos2_t[:]), gates[m][:, 1, :], MULT)
-            nc.vector.tensor_add(total[:], first[:], second[:])
-            nc.sync.dma_start(out=out[m * P : (m + 1) * P, :], in_=total[:])
+            if m == 0:
+                nc.vector.tensor_tensor(second[:], y[m][:].indirect(pos2_t[:]), gates[m][:, 1, :], MULT)
+            else:
+                for h in range(2):
+                    nc.vector.tensor_tensor(
+                        second[:, halves[h]],
+                        y[m][:].indirect(pos2_t[:, h * HALF // 16 : (h + 1) * HALF // 16]),
+                        gates[m][:, 1, halves[h]],
+                        MULT,
+                    )
+            products.append((first, second))
+
+        both = [sums.tile([P, HALF], F32, name="both") for h in range(2)]
+        for k in range(2):
+            for h in range(2):
+                nc.tensor.matmul(both[h][:], identity[:], products[0][k][:, halves[h]], start=(k == 0), stop=(k == 1))
+        total = keep.tile([P, T], F32, name="total0")
+        for h in range(2):
+            nc.scalar.copy(total[:, halves[h]], both[h][:])
+        nc.scalar.dma_start(out=out[0:P, :], in_=total[:])
+
+        first, second = products[1]
+        for h in range(2):
+            total = keep.tile([P, HALF], F32, name=f"total1{h}")
+            nc.vector.tensor_add(total[:], first[:, halves[h]], second[:, halves[h]])
+            nc.sync.dma_start(out=out[P:N, halves[h]], in_=total[:])

@@ -22,7 +22,7 @@ PASSES = K // (P * PACK)
 BLOCKS = N // P
 HALF = T // 2
 SLOTS = E * C
-CHUNKS = (((0, 384), (384, 512)), ((0, 256), (256, 512)))
+CHUNKS = (((0, 512),), ((0, 512),))
 PIECES = ((0, 3), (3, 6), (6, 8))
 
 
@@ -110,15 +110,14 @@ def tile_routed_moe_kernel(tc, xT, w_words, w_scales, b, gate, offs, pos1, pos2,
                 in_=src[:].indirect(offs_t[:, e0 * C // 16 : e1 * C // 16]),
             )
 
+        interleave(nc.scalar.copy, 0, 0, 352, 512)
         interleave(nc.vector.tensor_copy, 0, 0, 0, 256)
-        interleave(nc.scalar.copy, 0, 0, 256, 384)
+        interleave(nc.vector.tensor_copy, 0, 0, 256, 352)
         quantise(0, 0, 256)
-        quantise(0, 256, 384)
-        interleave(nc.vector.tensor_copy, 0, 1, 384, 464)
-        interleave(nc.scalar.copy, 0, 1, 464, 512)
-        quantise(0, 384, 512)
+        quantise(0, 256, 512)
         interleave(nc.scalar.copy, 1, 0, 0, 256)
-        interleave(nc.scalar.copy, 1, 1, 256, 512)
+        interleave(nc.scalar.copy, 1, 0, 256, 432)
+        interleave(nc.vector.tensor_copy, 1, 0, 432, 512)
         for e0, e1 in PIECES:
             gather(slot_codes[0], x_codes[0], e0, e1)
         quantise(1, 0, HALF)

@@ -82,9 +82,12 @@ def tile_routed_moe_kernel(tc, xT, w_words, w_scales, b, gate, offs, pos1, pos2,
         nc.sync.dma_start(pos2_t[:], pos2)
         gates = []
         for m in range(BLOCKS):
-            g = keep.tile([P, 2, T], F32, name=f"gate{m}")
-            nc.sync.dma_start(out=g[:], in_=gate[:, m * P : (m + 1) * P, :].rearrange("r p t -> p r t"))
-            gates.append(g)
+            pair = []
+            for r in range(2):
+                g = keep.tile([P, T], F32, name=f"gate{m}{r}")
+                nc.sync.dma_start(out=g[:], in_=gate[r, m * P : (m + 1) * P, :])
+                pair.append(g)
+            gates.append(pair)
 
         x_bf = [keep.tile([P, T, PACK], BF16, name=f"x_bf{a}", align_bytes=64) for a in range(PASSES)]
         x_codes = [keep.tile([P, T], U32, name=f"x_codes{a}", align_bytes=64) for a in range(PASSES)]
@@ -126,7 +129,11 @@ def tile_routed_moe_kernel(tc, xT, w_words, w_scales, b, gate, offs, pos1, pos2,
         y = [keep.tile([P, SLOTS], F32, name=f"y{m}") for m in range(BLOCKS)]
         for e0, e1 in PIECES:
             gather(slot_planes, x_planes, e0, e1)
-            gather(slot_codes[1], x_codes[1], e0, e1)
+            if e1 < E:
+                gather(slot_codes[1], x_codes[1], e0, e1)
+            else:
+                for e in range(e0, e1):
+                    gather(slot_codes[1], x_codes[1], e, e + 1)
             groups = [(m, e) for m in range(BLOCKS) for e in range(e0, e1)]
             banks = {}
             for a in range(PASSES):
@@ -148,35 +155,24 @@ def tile_routed_moe_kernel(tc, xT, w_words, w_scales, b, gate, offs, pos1, pos2,
                 slots = slice(e * C, (e + 1) * C)
                 nc.scalar.activation(y[m][:, slots], banks[m, e][:], ACT.Gelu_apprx_tanh, bias=bias[:, m, e : e + 1])
 
-        halves = [slice(h * HALF, (h + 1) * HALF) for h in range(2)]
         products = []
         for m in range(BLOCKS):
             first = keep.tile([P, T], F32, name=f"first{m}")
             second = keep.tile([P, T], F32, name=f"second{m}")
-            nc.vector.tensor_tensor(first[:], y[m][:].indirect(pos1_t[:]), gates[m][:, 0, :], MULT)
-            if m == 0:
-                nc.vector.tensor_tensor(second[:], y[m][:].indirect(pos2_t[:]), gates[m][:, 1, :], MULT)
-            else:
-                for h in range(2):
-                    nc.vector.tensor_tensor(
-                        second[:, halves[h]],
-                        y[m][:].indirect(pos2_t[:, h * HALF // 16 : (h + 1) * HALF // 16]),
-                        gates[m][:, 1, halves[h]],
-                        MULT,
-                    )
+            nc.vector.tensor_tensor(first[:], y[m][:].indirect(pos1_t[:]), gates[m][0][:], MULT)
+            nc.vector.tensor_tensor(second[:], y[m][:].indirect(pos2_t[:]), gates[m][1][:], MULT)
             products.append((first, second))
 
-        both = [sums.tile([P, HALF], F32, name="both") for h in range(2)]
+        tensor_cols = (slice(0, 192), slice(192, 384))
+        both = [sums.tile([P, 192], F32, name="both") for cols in tensor_cols]
         for k in range(2):
-            for h in range(2):
-                nc.tensor.matmul(both[h][:], identity[:], products[0][k][:, halves[h]], start=(k == 0), stop=(k == 1))
-        total = keep.tile([P, T], F32, name="total0")
-        for h in range(2):
-            nc.scalar.copy(total[:, halves[h]], both[h][:])
-        nc.scalar.dma_start(out=out[0:P, :], in_=total[:])
-
-        first, second = products[1]
-        for h in range(2):
-            total = keep.tile([P, HALF], F32, name=f"total1{h}")
-            nc.vector.tensor_add(total[:], first[:, halves[h]], second[:, halves[h]])
-            nc.sync.dma_start(out=out[P:N, halves[h]], in_=total[:])
+            for acc, cols in zip(both, tensor_cols):
+                nc.tensor.matmul(acc[:], identity[:], products[0][k][:, cols], start=(k == 0), stop=(k == 1))
+        for h, cols in enumerate(tensor_cols):
+            total = keep.tile([P, 192], F32, name=f"tensor_total{h}")
+            nc.scalar.copy(total[:], both[h][:])
+            nc.scalar.dma_start(out=out[0:P, cols], in_=total[:])
+        for m, lo, hi in ((0, 384, 512), (1, 0, 320), (1, 320, 512)):
+            total = keep.tile([P, hi - lo], F32, name=f"vector_total{m}_{lo}")
+            nc.vector.tensor_add(total[:], products[m][0][:, lo:hi], products[m][1][:, lo:hi])
+            nc.sync.dma_start(out=out[m * P : (m + 1) * P, lo:hi], in_=total[:])

from contextlib import ExitStack

import concourse.mybir as mybir
from concourse.masks import make_identity

K, T, E, C, N = 1024, 512, 8, 128, 256
FLOPS = 2 * K * N * E * C

F32 = mybir.dt.float32
BF16 = mybir.dt.bfloat16
U32 = mybir.dt.uint32
I32 = mybir.dt.int32
U16 = mybir.dt.uint16
U8 = mybir.dt.uint8
FP8X4 = mybir.dt.float8_e4m3fn_x4
ACT = mybir.ActivationFunctionType
MULT = mybir.AluOpType.mult

P = 128
PACK = 4
PASSES = K // (P * PACK)
BLOCKS = N // P
HALF = T // 2
SLOTS = E * C
CHUNKS = (((0, 512),), ((0, 512),))
PIECES = ((0, 3), (3, 6), (6, 8))


def tile_routed_moe_kernel(tc, xT, w_words, w_scales, b, gate, offs, pos1, pos2, out):
    nc = tc.nc
    with ExitStack() as ctx:
        keep = ctx.enter_context(tc.tile_pool(name="keep", bufs=1))
        psum = ctx.enter_context(tc.psum_pool(name="psum", bufs=6))
        sums = ctx.enter_context(tc.psum_pool(name="sums", bufs=2))

        offs_t = keep.tile([P, SLOTS // 16], U16, name="offs_t")
        pos1_t = keep.tile([P, T // 16], U16, name="pos1_t")
        pos2_t = keep.tile([P, T // 16], U16, name="pos2_t")
        bias = keep.tile([P, BLOCKS, E], F32, name="bias")
        w_codes = keep.tile([P, E * PASSES, N], U32, name="w_codes", align_bytes=64)
        w_planes = keep.tile([P, E * PASSES, N], U8, name="w_planes", align_bytes=64)
        x_planes = keep.tile([P, T], U8, name="x_planes", align_bytes=64)
        slot_planes = keep.tile([P, SLOTS], U8, name="slot_planes", align_bytes=64)

        warm = keep.tile([P, 1], F32, name="warm")
        nc.gpsimd.memset(warm[:], 0.0)
        warmed = keep.tile([P, 1], F32, name="warmed")
        nc.scalar.activation(warmed[:], warm[:], ACT.Gelu_apprx_tanh)

        nc.gpsimd.memset(x_planes[:], 0)
        identity = keep.tile([P, P], F32, name="identity")
        make_identity(nc, identity[:])
        nc.vector.memset(w_planes[:].rearrange("p g n -> p (g n)").bitcast(I32), 0)

        xv = xT.rearrange("(a p j) t -> a p j t", p=P, j=PACK)
        raw = []
        for a in range(PASSES):
            chunks = []
            for lo, hi in CHUNKS[a]:
                r = keep.tile([P, PACK, hi - lo], F32, name=f"raw{a}_{lo}")
                nc.sync.dma_start(out=r[:], in_=xv[a, :, :, lo:hi])
                chunks.append(r)
            raw.append(chunks)
            if a == 0:
                nc.sync.dma_start(offs_t[:], offs)

        wsv = w_scales.rearrange("e a q n -> q (e a) n")
        for quad in range(4):
            nc.sync.dma_start(
                out=w_planes[32 * quad : 32 * quad + 4, :, :].bitcast(I32),
                in_=wsv[4 * quad : 4 * quad + 4].bitcast(I32),
            )
        wwv = w_words.rearrange("e a p n r -> p (e a) (n r)")
        for e0, e1 in PIECES:
            nc.sync.dma_start(
                out=w_codes[:, e0 * PASSES : e1 * PASSES, :].bitcast(I32),
                in_=wwv[:, e0 * PASSES : e1 * PASSES, :].bitcast(I32),
            )
            if e0 == 0:
                nc.sync.dma_start(out=bias[:], in_=b.rearrange("(m p) e -> p m e", p=P))
        nc.sync.dma_start(pos1_t[:], pos1)
        nc.sync.dma_start(pos2_t[:], pos2)
        gates = []
        for m in range(BLOCKS):
            pair = []
            for r in range(2):
                g = keep.tile([P, T], F32, name=f"gate{m}{r}")
                nc.sync.dma_start(out=g[:], in_=gate[r, m * P : (m + 1) * P, :])
                pair.append(g)
            gates.append(pair)

        x_bf = [keep.tile([P, T, PACK], BF16, name=f"x_bf{a}", align_bytes=64) for a in range(PASSES)]
        x_codes = [keep.tile([P, T], U32, name=f"x_codes{a}", align_bytes=64) for a in range(PASSES)]
        slot_codes = [keep.tile([P, SLOTS], U32, name=f"slot_codes{a}", align_bytes=64) for a in range(PASSES)]

        def interleave(copy, a, h, lo, hi):
            start = CHUNKS[a][h][0]
            copy(
                out=x_bf[a][:, lo:hi, :].rearrange("p (c i) j -> p c j i", i=4),
                in_=raw[a][h][:, :, lo - start : hi - start].rearrange("p j (c i) -> p c j i", i=4),
            )

        def quantise(a, lo, hi):
            nc.vector.quantize_mx(
                out=x_codes[a][:, lo:hi].bitcast(FP8X4),
                scales=x_planes[4 * a : P, lo:hi],
                in_=x_bf[a][:, lo:hi, :].rearrange("p t j -> p (t j)"),
            )

        def gather(dst, src, e0, e1):
            nc.vector.tensor_copy(
                out=dst[:, e0 * C : e1 * C],
                in_=src[:].indirect(offs_t[:, e0 * C // 16 : e1 * C // 16]),
            )

        interleave(nc.scalar.copy, 0, 0, 352, 512)
        interleave(nc.vector.tensor_copy, 0, 0, 0, 256)
        interleave(nc.vector.tensor_copy, 0, 0, 256, 352)
        quantise(0, 0, 256)
        quantise(0, 256, 512)
        interleave(nc.scalar.copy, 1, 0, 0, 256)
        interleave(nc.scalar.copy, 1, 0, 256, 432)
        interleave(nc.vector.tensor_copy, 1, 0, 432, 512)
        for e0, e1 in PIECES:
            gather(slot_codes[0], x_codes[0], e0, e1)
        quantise(1, 0, HALF)
        quantise(1, HALF, T)

        y = [keep.tile([P, SLOTS], F32, name=f"y{m}") for m in range(BLOCKS)]
        for e0, e1 in PIECES:
            gather(slot_planes, x_planes, e0, e1)
            if e1 < E:
                gather(slot_codes[1], x_codes[1], e0, e1)
            else:
                for e in range(e0, e1):
                    gather(slot_codes[1], x_codes[1], e, e + 1)
            groups = [(m, e) for m in range(BLOCKS) for e in range(e0, e1)]
            banks = {}
            for a in range(PASSES):
                for m, e in groups:
                    slots = slice(e * C, (e + 1) * C)
                    rows = slice(m * P, (m + 1) * P)
                    if a == 0:
                        banks[m, e] = psum.tile([P, C], F32, name="acc")
                    nc.tensor.matmul_mx(
                        out=banks[m, e][:],
                        lhsT=w_codes[:, e * PASSES + a, rows].bitcast(FP8X4),
                        lhsT_scale=w_planes[:, e * PASSES + a, rows],
                        rhs=slot_codes[a][:, slots].bitcast(FP8X4),
                        rhs_scale=slot_planes[4 * a : P, slots],
                        start=(a == 0),
                        stop=(a == PASSES - 1),
                    )
            for m, e in groups:
                slots = slice(e * C, (e + 1) * C)
                nc.scalar.activation(y[m][:, slots], banks[m, e][:], ACT.Gelu_apprx_tanh, bias=bias[:, m, e : e + 1])

        products = []
        for m in range(BLOCKS):
            first = keep.tile([P, T], F32, name=f"first{m}")
            second = keep.tile([P, T], F32, name=f"second{m}")
            nc.vector.tensor_tensor(first[:], y[m][:].indirect(pos1_t[:]), gates[m][0][:], MULT)
            nc.vector.tensor_tensor(second[:], y[m][:].indirect(pos2_t[:]), gates[m][1][:], MULT)
            products.append((first, second))

        tensor_cols = (slice(0, 192), slice(192, 384))
        both = [sums.tile([P, 192], F32, name="both") for cols in tensor_cols]
        for k in range(2):
            for acc, cols in zip(both, tensor_cols):
                nc.tensor.matmul(acc[:], identity[:], products[0][k][:, cols], start=(k == 0), stop=(k == 1))
        for h, cols in enumerate(tensor_cols):
            total = keep.tile([P, 192], F32, name=f"tensor_total{h}")
            nc.scalar.copy(total[:], both[h][:])
            nc.scalar.dma_start(out=out[0:P, cols], in_=total[:])
        for m, lo, hi in ((0, 384, 512), (1, 0, 320), (1, 320, 512)):
            total = keep.tile([P, hi - lo], F32, name=f"vector_total{m}_{lo}")
            nc.vector.tensor_add(total[:], products[m][0][:, lo:hi], products[m][1][:, lo:hi])
            nc.sync.dma_start(out=out[m * P : (m + 1) * P, lo:hi], in_=total[:])
